import numpy as np
import ml_dtypes


def mxq(x, axis, fmt="e4m3"):
    dtype, down = {"e4m3": (ml_dtypes.float8_e4m3fn, 7), "e5m2": (ml_dtypes.float8_e5m2, 14)}[fmt]
    v = np.moveaxis(np.asarray(x, np.float32).astype(ml_dtypes.bfloat16).astype(np.float64), axis, -1)
    blocks = v.reshape(v.shape[:-1] + (-1, 32))
    amax = np.abs(blocks).max(-1, keepdims=True)
    byte = np.maximum(np.where(amax > 0, np.frexp(amax)[1] - 1 + 127, 0) - down, 1)
    scale = np.exp2(byte - 127.0)
    codes = (blocks / scale).astype(np.float32).astype(dtype).astype(np.float64)
    return np.moveaxis((codes * scale).reshape(v.shape), -1, axis)


WIDE = False


def mx_kscale(k):
    if not WIDE:
        return np.ones(k)
    levels = np.array([10, -10, 5, -5, 0])
    if k % 512:
        return np.exp2(np.random.permutation(np.resize(levels, k // 32))).repeat(32)
    a = np.empty((k // 512, 16))
    for p in range(k // 512):
        a[p, :8] = np.random.permutation(np.resize(levels, 8))
        for g in range(8):
            far = levels[np.abs(levels - a[p, g]) >= 10]
            a[p, g + 8] = far[np.random.randint(len(far))]
    return np.exp2(a.ravel()).repeat(32)


def f64(x):
    return np.asarray(x).astype(np.float64)


def striped(idx):
    return np.tile(np.asarray(idx).reshape(-1, 16).T, (8, 1)).astype(np.uint16)


def unstriped(offs):
    return offs[:16].T.reshape(-1).astype(np.int64)


E2M1 = np.array([0.0, 0.5, 1.0, 1.5, 2.0, 3.0, 4.0, 6.0, -0.0, -0.5, -1.0, -1.5, -2.0, -3.0, -4.0, -6.0])


def pack_weight(w, fmt):
    k, n = w.shape
    w = f64(np.asarray(w, np.float32).astype(ml_dtypes.bfloat16)).reshape(k // 32, 32, n)
    amax = np.abs(w).max(1)
    if fmt == "e4m3":
        byte = np.frexp(amax)[1] - 1 + 127 - 7
    else:
        mant, ex = np.frexp(amax / 6.0)
        byte = np.where(mant > 0.5, ex, ex - 1) + 127
    byte = np.clip(np.where(amax > 0, byte, 1), 1, 254)
    scaled = (w * np.exp2(127.0 - byte)[:, None, :]).reshape(k, n).astype(np.float32)
    by_word = np.ascontiguousarray(scaled.reshape(k // 512, 128, 4, n).transpose(0, 1, 3, 2))
    if fmt == "e4m3":
        words = by_word.astype(ml_dtypes.float8_e4m3fn).view(np.uint8)
    else:
        c = by_word.astype(ml_dtypes.float4_e2m1fn).view(np.uint8) & 0xF
        words = (c[..., 0::2] | (c[..., 1::2] << 4)).reshape(k // 512, 128, 2 * n)
    return np.ascontiguousarray(words), np.ascontiguousarray(byte.astype(np.uint8).reshape(k // 512, 16, n))


def unpack_weight(words, scales, fmt):
    g, _, n = scales.shape
    words = np.ascontiguousarray(words).reshape(g, 128, n, -1)
    if fmt == "e4m3":
        vals = words.view(ml_dtypes.float8_e4m3fn).astype(np.float64)
    else:
        nib = np.empty((g, 128, n, 4), np.uint8)
        nib[..., 0::2] = words & 0xF
        nib[..., 1::2] = words >> 4
        vals = E2M1[nib]
    vals = vals * np.repeat(np.exp2(scales.astype(np.float64) - 127.0), 8, axis=1)[..., None]
    return vals.transpose(0, 1, 3, 2).reshape(g * 512, n)


def sigmoid(v):
    return 1.0 / (1.0 + np.exp(-v))


K, R, F, T, J, G = 512, 128, 512, 2048, 512, 32


def setup_inputs():
    n = np.random.standard_normal
    idx = np.random.permutation(T)[:J]
    fk = mx_kscale(K)
    ff = mx_kscale(F)
    tabp = pack_weight(n((K, T)) / fk[:, None], "e2m1")
    return {
        "tab_words": tabp[0],
        "tab_scales": tabp[1],
        "w1": (n((K, R)) * 1 / np.sqrt(K) * fk[:, None]).astype(np.float32),
        "steep": (np.random.uniform(1.0, 4.0, (R, 1))).astype(np.float32),
        "bias": (np.random.uniform(-0.5, 0.5, (R, 1))).astype(np.float32),
        "wo": (n((F, R)) * 1 / np.sqrt(F) * ff[:, None]).astype(np.float32),
        "dy": (n((F, J)) / ff[:, None]).astype(np.float32),
        "og": (np.random.uniform(0.3, 1.0, (R, 1))).astype(np.float32),
        "base": (0.3 * n((R, J))).astype(np.float32),
        "offs": striped(idx),
    }


def reference(tab_words, tab_scales, w1, steep, bias, wo, dy, og, base, offs):
    idx = unstriped(offs)
    tabu = unpack_weight(tab_words, tab_scales, "e2m1")
    w1q = mxq(f64(w1), 0, "e4m3")
    tabidxg = tabu[:, idx]
    a = w1q.T @ tabidxg
    m1 = a.reshape(R, G, J // G).mean(axis=2)
    gt = sigmoid(m1 * f64(steep) + f64(bias))
    gr0 = np.repeat(gt, J // G, axis=1)
    woq = mxq(f64(wo), 0, "e4m3")
    dyq = mxq(f64(dy), 0, "e4m3")
    c0 = woq.T @ dyq
    dgr0 = c0 * a
    dgt = dgr0.reshape(R, G, J // G).sum(axis=2)
    dm1 = dgt * gt * (1.0 - gt) * f64(steep)
    e1 = dm1 / 16.0
    r1 = np.repeat(e1, J // G, axis=1)
    da = c0 * gr0 + r1
    hda = da * 2.0
    he1 = hda.reshape(R, G, J // G).sum(axis=2)
    hdm1 = he1 / 16.0
    hdgt = hdm1 * f64(steep) * (1.0 - gt) * gt
    r51 = np.repeat(hdgt, J // G, axis=1)
    hgr0 = hda * c0
    hgt = hdm1 * f64(steep) * (1.0 - gt) * dgt + hgr0.reshape(R, G, J // G).sum(axis=2) - hdm1 * f64(steep) * dgt * gt
    hm1 = hgt * gt * (1.0 - gt) * f64(steep)
    e52 = hm1 / 16.0
    r52 = np.repeat(e52, J // G, axis=1)
    ha = r51 * c0 + r52
    y = ha * f64(og) + f64(base)
    return y

@@ -1,0 +1,190 @@
+from contextlib import ExitStack
+
+import concourse.mybir as mybir
+
+K, R, F, T, J, G = 512, 128, 512, 2048, 512, 32
+FLOPS = 2 * K * R * J + 2 * F * R * J
+
+F32 = mybir.dt.float32
+BF16 = mybir.dt.bfloat16
+I32 = mybir.dt.int32
+U32 = mybir.dt.uint32
+U16 = mybir.dt.uint16
+U8 = mybir.dt.uint8
+FP8X4 = mybir.dt.float8_e4m3fn_x4
+FP4X4 = mybir.dt.float4_e2m1fn_x4
+ACT = mybir.ActivationFunctionType
+ALU = mybir.AluOpType
+AX = mybir.AxisListType
+
+P = 128
+PACK = 4
+S = J // G
+HALVES = 2
+JH = J // HALVES
+GH = G // HALVES
+DY_VECTOR = 160
+
+
+def interleave_views(grouped, raw):
+    return (
+        grouped.rearrange("p (c i) t -> p c t i", i=4),
+        raw.rearrange("p t (c i) -> p c t i", i=4),
+    )
+
+
+def tile_attend_gpsqueeze_kernel(tc, tab_words, tab_scales, w1, steep, bias, wo, dy, og, base, offs, out):
+    nc = tc.nc
+    with ExitStack() as ctx:
+        sb = ctx.enter_context(tc.tile_pool(name="sb", bufs=1))
+        ps = ctx.enter_context(tc.psum_pool(name="ps", bufs=1))
+
+        offsets = sb.tile([P, J // 16], U16, name="offsets")
+        words = sb.tile([P, T], U16, name="words", align_bytes=64)
+        sbytes = sb.tile([P, T], U8, name="sbytes", align_bytes=64)
+        w1_raw = sb.tile([P, PACK, R], F32, name="w1_raw", align_bytes=64)
+        wo_raw = sb.tile([P, PACK, R], F32, name="wo_raw", align_bytes=64)
+        dy_raw = [sb.tile([P, PACK, JH], F32, name="dy_raw%d" % h, align_bytes=64) for h in range(HALVES)]
+        base_sb = sb.tile([P, J], F32, name="base_sb", align_bytes=64)
+        steep_sb = sb.tile([P, 1], F32, name="steep_sb")
+        bias_sb = sb.tile([P, 1], F32, name="bias_sb")
+        og_sb = sb.tile([P, 1], F32, name="og_sb")
+
+        nc.vector.memset(sbytes[:].bitcast(I32), 0)
+        nc.sync.dma_start(offsets[:], offs)
+        nc.sync.dma_start(words[:].bitcast(I32), tab_words[0].bitcast(I32))
+        for r in range(4):
+            nc.sync.dma_start(sbytes[r:P:32, :].bitcast(I32), tab_scales[0][r:16:4, :].bitcast(I32))
+        nc.sync.dma_start(w1_raw[:], w1.rearrange("(p t) r -> p t r", t=PACK))
+        nc.sync.dma_start(wo_raw[:], wo.rearrange("(p t) r -> p t r", t=PACK))
+        nc.gpsimd.dma_start(steep_sb[:], steep)
+        nc.gpsimd.dma_start(bias_sb[:], bias)
+        dy_view = dy.rearrange("(p t) j -> p t j", t=PACK)
+        for h in range(HALVES):
+            nc.sync.dma_start(dy_raw[h][:], dy_view[:, :, h * JH : (h + 1) * JH])
+        nc.sync.dma_start(og_sb[:], og)
+        nc.sync.dma_start(base_sb[:], base)
+
+        slopes = (-1.0 / 64, -0.5, -1.0 / 16, -3.0 / 32)
+        levels = (1.0 / 64, 0.5, 0.0, 1.0 / 32)
+        powers = sb.tile([P, 2, 4], F32, name="powers")
+        line = sb.tile([P, 2, 5], F32, name="line")
+        for n in range(4):
+            nc.gpsimd.memset(powers[:, 0, n : n + 1], slopes[n])
+            nc.gpsimd.memset(powers[:, 1, n : n + 1], levels[n])
+        nc.gpsimd.memset(line[:, :, 0:1], 1.0)
+        half_bias = sb.tile([P, 1], F32, name="half_bias")
+        nc.gpsimd.tensor_scalar(line[:, :, 1:5], powers[:], steep_sb[:], 0.0, ALU.mult, ALU.add)
+        nc.gpsimd.tensor_scalar(half_bias[:], bias_sb[:], 0.5, 0.0, ALU.mult, ALU.add)
+
+        g_words = sb.tile([P, J], U16, name="g_words", align_bytes=64)
+        g_bytes = sb.tile([P, J], U8, name="g_bytes", align_bytes=64)
+        nc.vector.tensor_copy(g_words[:], words[:].indirect(offsets[:]))
+        nc.vector.tensor_copy(g_bytes[:], sbytes[:].indirect(offsets[:]))
+
+        def quantise(name, grouped, width):
+            codes = sb.tile([P, width], U32, name=name + "_codes", align_bytes=64)
+            scales = sb.tile([P, width], U8, name=name + "_scales", align_bytes=64)
+            nc.vector.quantize_mx(
+                out=codes[:].bitcast(FP8X4), scales=scales[:], in_=grouped[:].rearrange("p c t -> p (c t)")
+            )
+            return codes, scales
+
+        w1_bf = sb.tile([P, R, PACK], BF16, name="w1_bf", align_bytes=64)
+        dst, src = interleave_views(w1_bf[:], w1_raw[:])
+        nc.scalar.activation(dst, src, ACT.Copy)
+        w1_codes, w1_scales = quantise("w1", w1_bf, R)
+
+        a_ps = [ps.tile([P, JH], F32, name="a_ps%d" % h) for h in range(HALVES)]
+        for h in range(HALVES):
+            cols = slice(h * JH, (h + 1) * JH)
+            nc.tensor.matmul_mx(
+                out=a_ps[h][:], lhsT=w1_codes[:].bitcast(FP8X4), lhsT_scale=w1_scales[:],
+                rhs=g_words[:, cols].bitcast(FP4X4), rhs_scale=g_bytes[:, cols], start=True, stop=True,
+            )
+
+        wo_bf = sb.tile([P, R, PACK], BF16, name="wo_bf", align_bytes=64)
+        dst, src = interleave_views(wo_bf[:], wo_raw[:])
+        nc.scalar.copy(dst, src)
+        wo_codes, wo_scales = quantise("wo", wo_bf, R)
+
+        dy_bf = [sb.tile([P, JH, PACK], BF16, name="dy_bf%d" % h, align_bytes=64) for h in range(HALVES)]
+
+        def round_dy(h):
+            dst, src = interleave_views(dy_bf[h][:, 0:DY_VECTOR, :], dy_raw[h][:, :, 0:DY_VECTOR])
+            nc.vector.tensor_copy(dst, src)
+            dst, src = interleave_views(dy_bf[h][:, DY_VECTOR:JH, :], dy_raw[h][:, :, DY_VECTOR:JH])
+            nc.scalar.copy(dst, src)
+
+        round_dy(0)
+
+        sum_a = sb.tile([P, G], F32, name="sum_a")
+        a_sb = sb.tile([P, J], F32, name="a_sb")
+        nc.scalar.copy(a_sb[:, 0:JH], a_ps[0][:])
+        nc.vector.tensor_reduce(sum_a[:, GH:G], a_ps[1][:].rearrange("p (g s) -> p g s", s=S), AX.X, ALU.add)
+        nc.vector.tensor_reduce(sum_a[:, 0:GH], a_ps[0][:].rearrange("p (g s) -> p g s", s=S), AX.X, ALU.add)
+        nc.scalar.copy(a_sb[:, JH:J], a_ps[1][:])
+        th = sb.tile([P, G], F32, name="th")
+        nc.scalar.activation(th[:], sum_a[:], ACT.Tanh, bias=half_bias[:], scale=line[:, 1, 4:5])
+
+        round_dy(1)
+
+        gate = sb.tile([P, 7, G], F32, name="gate")
+        coef = sb.tile([P, 6, G], F32, name="coef")
+        for n in range(5):
+            nc.scalar.activation(
+                gate[:, 2 + n, :], th[:], ACT.Identity, bias=line[:, 1, n : n + 1], scale=line[:, 0, n : n + 1]
+            )
+        nc.vector.tensor_tensor(
+            gate[:, 0:2, :], gate[:, 3:5, :], gate[:, 2:3, :].to_broadcast([P, 2, G]), ALU.mult
+        )
+        nc.vector.tensor_tensor(
+            coef[:, 2:4, :], gate[:, 1:3, :], gate[:, 0:1, :].to_broadcast([P, 2, G]), ALU.mult
+        )
+        nc.vector.tensor_tensor(coef[:, 0:2, :], coef[:, 2:4, :], gate[:, 5:7, :], ALU.mult)
+
+        for h in range(HALVES):
+            cols = slice(h * JH, (h + 1) * JH)
+            groups = slice(h * GH, (h + 1) * GH)
+            dy_codes, dy_scales = quantise("dy%d" % h, dy_bf[h], JH)
+            c_ps = ps.tile([P, JH], F32, name="c_ps%d" % h)
+            nc.tensor.matmul_mx(
+                out=c_ps[:], lhsT=wo_codes[:].bitcast(FP8X4), lhsT_scale=wo_scales[:],
+                rhs=dy_codes[:].bitcast(FP8X4), rhs_scale=dy_scales[:], start=True, stop=True,
+            )
+            c_grouped = c_ps[:].rearrange("p (g s) -> p g s", s=S)
+            prods = sb.tile([P, 2, JH], F32, name="prods%d" % h)
+            sums = sb.tile([P, 3, GH], F32, name="sums%d" % h)
+            nc.scalar.activation(prods[:, 0, :], c_ps[:], ACT.Square)
+            nc.vector.tensor_tensor(prods[:, 1, :], c_ps[:], a_sb[:, cols], ALU.mult)
+            nc.vector.tensor_reduce(sums[:, 2, :], c_grouped, AX.X, ALU.add)
+            nc.vector.tensor_reduce(
+                sums[:, 0:2, :].rearrange("p i g -> p (i g)"),
+                prods[:].rearrange("p i (g s) -> p (i g) s", s=S), AX.X, ALU.add,
+            )
+            terms = sb.tile([P, 2, 2, GH], F32, name="terms%d" % h)
+            nc.vector.tensor_tensor(
+                terms[:],
+                coef[:, 0:4, groups].rearrange("p (o i) g -> p o i g", i=2),
+                sums[:, 1:3, :].unsqueeze(1).to_broadcast([P, 2, 2, GH]),
+                ALU.mult,
+            )
+            nc.vector.tensor_tensor(coef[:, 4:6, groups], terms[:, :, 0, :], terms[:, :, 1, :], ALU.add)
+            parts = sb.tile([P, 2, GH], F32, name="parts%d" % h)
+            nc.vector.tensor_tensor(parts[:], coef[:, 3:5, groups], sums[:, 0:2, :], ALU.mult)
+            scaled = sb.tile([P, GH, S], F32, name="scaled%d" % h)
+            nc.vector.scalar_tensor_tensor(
+                scaled[:], c_grouped, og_sb[:], coef[:, 5, groups].unsqueeze(2).to_broadcast([P, GH, S]),
+                ALU.mult, ALU.mult,
+            )
+            shift = sb.tile([P, GH], F32, name="shift%d" % h)
+            nc.vector.tensor_tensor(shift[:], parts[:, 0, :], parts[:, 1, :], ALU.add)
+            based = sb.tile([P, GH, S], F32, name="based%d" % h)
+            nc.vector.tensor_tensor(
+                based[:], scaled[:], base_sb[:, cols].rearrange("p (g s) -> p g s", s=S), ALU.add
+            )
+            result = sb.tile([P, GH, S], F32, name="result%d" % h)
+            nc.vector.scalar_tensor_tensor(
+                result[:], shift[:].unsqueeze(2).to_broadcast([P, GH, S]), og_sb[:], based[:], ALU.mult, ALU.add
+            )
+            nc.sync.dma_start(out[:, cols], result[:].rearrange("p g s -> p (g s)"))

@@ -23,7 +23,8 @@ S = J // G
 HALVES = 2
 JH = J // HALVES
 GH = G // HALVES
-DY_VECTOR = 160
+DY_SHARE = (128, 160)
+LATE = (R + JH) * PACK * 2
 
 
 def interleave_views(grouped, raw):
@@ -37,13 +38,14 @@ def tile_attend_gpsqueeze_kernel(tc, tab_words, tab_scales, w1, steep, bias, wo,
     nc = tc.nc
     with ExitStack() as ctx:
         sb = ctx.enter_context(tc.tile_pool(name="sb", bufs=1))
+        reuse = ctx.enter_context(tc.tile_pool(name="reuse", bufs=1))
         ps = ctx.enter_context(tc.psum_pool(name="ps", bufs=1))
 
         offsets = sb.tile([P, J // 16], U16, name="offsets")
         words = sb.tile([P, T], U16, name="words", align_bytes=64)
         sbytes = sb.tile([P, T], U8, name="sbytes", align_bytes=64)
         w1_raw = sb.tile([P, PACK, R], F32, name="w1_raw", align_bytes=64)
-        wo_raw = sb.tile([P, PACK, R], F32, name="wo_raw", align_bytes=64)
+        wo_raw = sb.tile([P, PACK, R], F32, name="wo_raw", tag="staged", align_bytes=64)
         dy_raw = [sb.tile([P, PACK, JH], F32, name="dy_raw%d" % h, align_bytes=64) for h in range(HALVES)]
         base_sb = sb.tile([P, J], F32, name="base_sb", align_bytes=64)
         steep_sb = sb.tile([P, 1], F32, name="steep_sb")
@@ -56,12 +58,12 @@ def tile_attend_gpsqueeze_kernel(tc, tab_words, tab_scales, w1, steep, bias, wo,
         for r in range(4):
             nc.sync.dma_start(sbytes[r:P:32, :].bitcast(I32), tab_scales[0][r:16:4, :].bitcast(I32))
         nc.sync.dma_start(w1_raw[:], w1.rearrange("(p t) r -> p t r", t=PACK))
-        nc.sync.dma_start(wo_raw[:], wo.rearrange("(p t) r -> p t r", t=PACK))
         nc.gpsimd.dma_start(steep_sb[:], steep)
         nc.gpsimd.dma_start(bias_sb[:], bias)
         dy_view = dy.rearrange("(p t) j -> p t j", t=PACK)
-        for h in range(HALVES):
-            nc.sync.dma_start(dy_raw[h][:], dy_view[:, :, h * JH : (h + 1) * JH])
+        nc.sync.dma_start(dy_raw[0][:], dy_view[:, :, 0:JH])
+        nc.sync.dma_start(wo_raw[:], wo.rearrange("(p t) r -> p t r", t=PACK))
+        nc.sync.dma_start(dy_raw[1][:], dy_view[:, :, JH:J])
         nc.sync.dma_start(og_sb[:], og)
         nc.sync.dma_start(base_sb[:], base)
 
@@ -71,11 +73,14 @@ def tile_attend_gpsqueeze_kernel(tc, tab_words, tab_scales, w1, steep, bias, wo,
         line = sb.tile([P, 2, 5], F32, name="line")
         for n in range(4):
             nc.gpsimd.memset(powers[:, 0, n : n + 1], slopes[n])
+        nc.scalar.activation(powers[:, 1, 0:2], powers[:, 0, 0:2], ACT.Copy, scale=-1.0)
+        for n in range(2, 4):
             nc.gpsimd.memset(powers[:, 1, n : n + 1], levels[n])
         nc.gpsimd.memset(line[:, :, 0:1], 1.0)
         half_bias = sb.tile([P, 1], F32, name="half_bias")
         nc.gpsimd.tensor_scalar(line[:, :, 1:5], powers[:], steep_sb[:], 0.0, ALU.mult, ALU.add)
         nc.gpsimd.tensor_scalar(half_bias[:], bias_sb[:], 0.5, 0.0, ALU.mult, ALU.add)
+
 
         g_words = sb.tile([P, J], U16, name="g_words", align_bytes=64)
         g_bytes = sb.tile([P, J], U8, name="g_bytes", align_bytes=64)
@@ -92,7 +97,7 @@ def tile_attend_gpsqueeze_kernel(tc, tab_words, tab_scales, w1, steep, bias, wo,
 
         w1_bf = sb.tile([P, R, PACK], BF16, name="w1_bf", align_bytes=64)
         dst, src = interleave_views(w1_bf[:], w1_raw[:])
-        nc.scalar.activation(dst, src, ACT.Copy)
+        nc.scalar.copy(dst, src)
         w1_codes, w1_scales = quantise("w1", w1_bf, R)
 
         a_ps = [ps.tile([P, JH], F32, name="a_ps%d" % h) for h in range(HALVES)]
@@ -103,31 +108,46 @@ def tile_attend_gpsqueeze_kernel(tc, tab_words, tab_scales, w1, steep, bias, wo,
                 rhs=g_words[:, cols].bitcast(FP4X4), rhs_scale=g_bytes[:, cols], start=True, stop=True,
             )
 
-        wo_bf = sb.tile([P, R, PACK], BF16, name="wo_bf", align_bytes=64)
-        dst, src = interleave_views(wo_bf[:], wo_raw[:])
-        nc.scalar.copy(dst, src)
-        wo_codes, wo_scales = quantise("wo", wo_bf, R)
+        first_bf = reuse.tile([P, R + JH, PACK], BF16, name="first_bf", align_bytes=64, offset=0)
 
-        dy_bf = [sb.tile([P, JH, PACK], BF16, name="dy_bf%d" % h, align_bytes=64) for h in range(HALVES)]
-
-        def round_dy(h):
-            dst, src = interleave_views(dy_bf[h][:, 0:DY_VECTOR, :], dy_raw[h][:, :, 0:DY_VECTOR])
-            nc.vector.tensor_copy(dst, src)
-            dst, src = interleave_views(dy_bf[h][:, DY_VECTOR:JH, :], dy_raw[h][:, :, DY_VECTOR:JH])
+        def round_on_scalar(grouped, raw):
+            dst, src = interleave_views(grouped, raw)
             nc.scalar.copy(dst, src)
 
-        round_dy(0)
+        round_on_scalar(first_bf[:, R + DY_SHARE[0] : R + JH, :], dy_raw[0][:, :, DY_SHARE[0] : JH])
+        dst, src = interleave_views(first_bf[:, R : R + DY_SHARE[0], :], dy_raw[0][:, :, 0 : DY_SHARE[0]])
+        nc.vector.tensor_copy(dst, src)
+        round_on_scalar(first_bf[:, 0:R, :], wo_raw[:])
+        first_codes, first_scales = quantise("first", first_bf, R + JH)
 
-        sum_a = sb.tile([P, G], F32, name="sum_a")
-        a_sb = sb.tile([P, J], F32, name="a_sb")
-        nc.scalar.copy(a_sb[:, 0:JH], a_ps[0][:])
-        nc.vector.tensor_reduce(sum_a[:, GH:G], a_ps[1][:].rearrange("p (g s) -> p g s", s=S), AX.X, ALU.add)
-        nc.vector.tensor_reduce(sum_a[:, 0:GH], a_ps[0][:].rearrange("p (g s) -> p g s", s=S), AX.X, ALU.add)
-        nc.scalar.copy(a_sb[:, JH:J], a_ps[1][:])
-        th = sb.tile([P, G], F32, name="th")
+        def product_with_dy(h, dy_codes, dy_scales):
+            bank = ps.tile([P, JH], F32, name="c_ps%d" % h)
+            nc.tensor.matmul_mx(
+                out=bank[:], lhsT=first_codes[:, 0:R].bitcast(FP8X4), lhsT_scale=first_scales[:, 0:R],
+                rhs=dy_codes.bitcast(FP8X4), rhs_scale=dy_scales, start=True, stop=True,
+            )
+            return bank
+
+        c_banks = [product_with_dy(0, first_codes[:, R : R + JH], first_scales[:, R : R + JH])]
+
+        sum_a = reuse.tile([P, G], F32, name="sum_a", align_bytes=64, offset=JH * PACK * 2)
+        a_sb = sb.tile([P, J], F32, name="a_sb", tag="staged", align_bytes=64)
+        for h in range(HALVES):
+            nc.scalar.copy(a_sb[:, h * JH : (h + 1) * JH], a_ps[h][:])
+            nc.vector.tensor_reduce(
+                sum_a[:, h * GH : (h + 1) * GH], a_ps[h][:].rearrange("p (g s) -> p g s", s=S), AX.X, ALU.add
+            )
+        th = reuse.tile([P, G], F32, name="th", align_bytes=64, offset=LATE)
         nc.scalar.activation(th[:], sum_a[:], ACT.Tanh, bias=half_bias[:], scale=line[:, 1, 4:5])
 
-        round_dy(1)
+        second_bf = reuse.tile([P, JH, PACK], BF16, name="second_bf", align_bytes=64, offset=0)
+        nc.gpsimd.tensor_scalar(
+            second_bf[:, 0 : DY_SHARE[1], :], dy_raw[1][:, :, 0 : DY_SHARE[1]].rearrange("p t c -> p c t"),
+            1.0, 0.0, ALU.mult, ALU.add,
+        )
+        round_on_scalar(second_bf[:, DY_SHARE[1] : JH, :], dy_raw[1][:, :, DY_SHARE[1] : JH])
+        second_codes, second_scales = quantise("second", second_bf, JH)
+        c_banks.append(product_with_dy(1, second_codes[:], second_scales[:]))
 
         gate = sb.tile([P, 7, G], F32, name="gate")
         coef = sb.tile([P, 6, G], F32, name="coef")
@@ -138,53 +158,55 @@ def tile_attend_gpsqueeze_kernel(tc, tab_words, tab_scales, w1, steep, bias, wo,
         nc.vector.tensor_tensor(
             gate[:, 0:2, :], gate[:, 3:5, :], gate[:, 2:3, :].to_broadcast([P, 2, G]), ALU.mult
         )
-        nc.vector.tensor_tensor(
-            coef[:, 2:4, :], gate[:, 1:3, :], gate[:, 0:1, :].to_broadcast([P, 2, G]), ALU.mult
+        nc.vector.scalar_tensor_tensor(
+            coef[:, 2:4, :], gate[:, 1:3, :], og_sb[:], gate[:, 0:1, :].to_broadcast([P, 2, G]), ALU.mult, ALU.mult
         )
         nc.vector.tensor_tensor(coef[:, 0:2, :], coef[:, 2:4, :], gate[:, 5:7, :], ALU.mult)
 
+        sums = sb.tile([P, 3, G], F32, name="sums")
+        c_grouped = []
+        squares = []
         for h in range(HALVES):
             cols = slice(h * JH, (h + 1) * JH)
             groups = slice(h * GH, (h + 1) * GH)
-            dy_codes, dy_scales = quantise("dy%d" % h, dy_bf[h], JH)
-            c_ps = ps.tile([P, JH], F32, name="c_ps%d" % h)
-            nc.tensor.matmul_mx(
-                out=c_ps[:], lhsT=wo_codes[:].bitcast(FP8X4), lhsT_scale=wo_scales[:],
-                rhs=dy_codes[:].bitcast(FP8X4), rhs_scale=dy_scales[:], start=True, stop=True,
-            )
-            c_grouped = c_ps[:].rearrange("p (g s) -> p g s", s=S)
-            prods = sb.tile([P, 2, JH], F32, name="prods%d" % h)
-            sums = sb.tile([P, 3, GH], F32, name="sums%d" % h)
-            nc.scalar.activation(prods[:, 0, :], c_ps[:], ACT.Square)
-            nc.vector.tensor_tensor(prods[:, 1, :], c_ps[:], a_sb[:, cols], ALU.mult)
-            nc.vector.tensor_reduce(sums[:, 2, :], c_grouped, AX.X, ALU.add)
+            c_ps = c_banks[h]
+            c_grouped.append(c_ps[:].rearrange("p (g s) -> p g s", s=S))
+            squares.append(reuse.tile([P, JH], F32, name="squares%d" % h, align_bytes=64, offset=LATE + (1 - h) * JH * 4))
+            prods = sb.tile([P, JH], F32, name="prods%d" % h)
+            nc.vector.tensor_tensor(prods[:], c_ps[:], a_sb[:, cols], ALU.mult)
+            nc.vector.tensor_reduce(sums[:, 2, groups], c_grouped[h], AX.X, ALU.add)
+            nc.scalar.activation(squares[h][:], c_ps[:], ACT.Square)
+            nc.vector.tensor_reduce(sums[:, 1, groups], prods[:].rearrange("p (g s) -> p g s", s=S), AX.X, ALU.add)
+
+        terms = sb.tile([P, 2, 2, G], F32, name="terms")
+        nc.vector.tensor_tensor(
+            terms[:],
+            coef[:, 0:4, :].rearrange("p (o i) g -> p o i g", i=2),
+            sums[:, 1:3, :].unsqueeze(1).to_broadcast([P, 2, 2, G]),
+            ALU.mult,
+        )
+        nc.vector.tensor_tensor(coef[:, 4:6, :], terms[:, :, 0, :], terms[:, :, 1, :], ALU.add)
+        for h in range(HALVES):
             nc.vector.tensor_reduce(
-                sums[:, 0:2, :].rearrange("p i g -> p (i g)"),
-                prods[:].rearrange("p i (g s) -> p (i g) s", s=S), AX.X, ALU.add,
+                sums[:, 0, h * GH : (h + 1) * GH], squares[h][:].rearrange("p (g s) -> p g s", s=S), AX.X, ALU.add
             )
-            terms = sb.tile([P, 2, 2, GH], F32, name="terms%d" % h)
-            nc.vector.tensor_tensor(
-                terms[:],
-                coef[:, 0:4, groups].rearrange("p (o i) g -> p o i g", i=2),
-                sums[:, 1:3, :].unsqueeze(1).to_broadcast([P, 2, 2, GH]),
-                ALU.mult,
-            )
-            nc.vector.tensor_tensor(coef[:, 4:6, groups], terms[:, :, 0, :], terms[:, :, 1, :], ALU.add)
-            parts = sb.tile([P, 2, GH], F32, name="parts%d" % h)
-            nc.vector.tensor_tensor(parts[:], coef[:, 3:5, groups], sums[:, 0:2, :], ALU.mult)
+        parts = sb.tile([P, 2, G], F32, name="parts")
+        nc.vector.tensor_tensor(parts[:], coef[:, 3:5, :], sums[:, 0:2, :], ALU.mult)
+        shift = sb.tile([P, G], F32, name="shift")
+        nc.vector.tensor_tensor(shift[:], parts[:, 0, :], parts[:, 1, :], ALU.add)
+        for h in range(HALVES):
+            cols = slice(h * JH, (h + 1) * JH)
+            groups = slice(h * GH, (h + 1) * GH)
             scaled = sb.tile([P, GH, S], F32, name="scaled%d" % h)
-            nc.vector.scalar_tensor_tensor(
-                scaled[:], c_grouped, og_sb[:], coef[:, 5, groups].unsqueeze(2).to_broadcast([P, GH, S]),
-                ALU.mult, ALU.mult,
-            )
-            shift = sb.tile([P, GH], F32, name="shift%d" % h)
-            nc.vector.tensor_tensor(shift[:], parts[:, 0, :], parts[:, 1, :], ALU.add)
             based = sb.tile([P, GH, S], F32, name="based%d" % h)
+            result = sb.tile([P, GH, S], F32, name="result%d" % h)
+            nc.vector.tensor_tensor(
+                scaled[:], c_grouped[h], coef[:, 5, groups].unsqueeze(2).to_broadcast([P, GH, S]), ALU.mult
+            )
             nc.vector.tensor_tensor(
                 based[:], scaled[:], base_sb[:, cols].rearrange("p (g s) -> p g s", s=S), ALU.add
             )
-            result = sb.tile([P, GH, S], F32, name="result%d" % h)
-            nc.vector.scalar_tensor_tensor(
-                result[:], shift[:].unsqueeze(2).to_broadcast([P, GH, S]), og_sb[:], based[:], ALU.mult, ALU.add
+            nc.vector.tensor_tensor(
+                result[:], based[:], shift[:, groups].unsqueeze(2).to_broadcast([P, GH, S]), ALU.add
             )
             nc.sync.dma_start(out[:, cols], result[:].rearrange("p g s -> p (g s)"))

@@ -23,40 +23,57 @@ S = J // G
 HALVES = 2
 JH = J // HALVES
 GH = G // HALVES
-DY_SHARE = (128, 160)
-LATE = (R + JH) * PACK * 2
+DY_FIRST_VECTOR = 128
+DY_SECOND_GPSIMD = 160
+GROUPS_SCALAR = 12
+
+FIRST_BF_BYTES = (R + JH) * PACK * 2
+SECOND_BF_BYTES = JH * PACK * 2
+SQUARES_BYTES = JH * 4
+AT_SUM_A = SECOND_BF_BYTES
+AT_GAINED = AT_SUM_A + G * 4
+AT_SQUARES = FIRST_BF_BYTES
+AT_TH = AT_SQUARES + SQUARES_BYTES - G * 2
 
 
-def interleave_views(grouped, raw):
+def interleave_views(rounded, raw):
     return (
-        grouped.rearrange("p (c i) t -> p c t i", i=4),
+        rounded.rearrange("p (c i) t -> p c t i", i=4),
         raw.rearrange("p t (c i) -> p c t i", i=4),
     )
+
+
+def by_group(flat):
+    return flat.rearrange("p (g s) -> p g s", s=S)
+
+
+def over_slots(per_group, count):
+    return per_group.unsqueeze(2).to_broadcast([P, count, S])
 
 
 def tile_attend_gpsqueeze_kernel(tc, tab_words, tab_scales, w1, steep, bias, wo, dy, og, base, offs, out):
     nc = tc.nc
     with ExitStack() as ctx:
         sb = ctx.enter_context(tc.tile_pool(name="sb", bufs=1))
-        reuse = ctx.enter_context(tc.tile_pool(name="reuse", bufs=1))
+        shared = ctx.enter_context(tc.tile_pool(name="shared", bufs=1))
         ps = ctx.enter_context(tc.psum_pool(name="ps", bufs=1))
 
         offsets = sb.tile([P, J // 16], U16, name="offsets")
         words = sb.tile([P, T], U16, name="words", align_bytes=64)
-        sbytes = sb.tile([P, T], U8, name="sbytes", align_bytes=64)
+        scale_bytes = sb.tile([P, T], U8, name="scale_bytes", align_bytes=64)
         w1_raw = sb.tile([P, PACK, R], F32, name="w1_raw", align_bytes=64)
-        wo_raw = sb.tile([P, PACK, R], F32, name="wo_raw", tag="staged", align_bytes=64)
+        wo_raw = sb.tile([P, PACK, R], F32, name="wo_raw", tag="wo_then_a", align_bytes=64)
         dy_raw = [sb.tile([P, PACK, JH], F32, name="dy_raw%d" % h, align_bytes=64) for h in range(HALVES)]
         base_sb = sb.tile([P, J], F32, name="base_sb", align_bytes=64)
         steep_sb = sb.tile([P, 1], F32, name="steep_sb")
         bias_sb = sb.tile([P, 1], F32, name="bias_sb")
         og_sb = sb.tile([P, 1], F32, name="og_sb")
 
-        nc.vector.memset(sbytes[:].bitcast(I32), 0)
-        nc.sync.dma_start(offsets[:], offs)
+        nc.vector.memset(scale_bytes[:].bitcast(I32), 0)
         nc.sync.dma_start(words[:].bitcast(I32), tab_words[0].bitcast(I32))
+        nc.sync.dma_start(offsets[:], offs)
         for r in range(4):
-            nc.sync.dma_start(sbytes[r:P:32, :].bitcast(I32), tab_scales[0][r:16:4, :].bitcast(I32))
+            nc.sync.dma_start(scale_bytes[r:P:32, :].bitcast(I32), tab_scales[0][r:16:4, :].bitcast(I32))
         nc.sync.dma_start(w1_raw[:], w1.rearrange("(p t) r -> p t r", t=PACK))
         nc.gpsimd.dma_start(steep_sb[:], steep)
         nc.gpsimd.dma_start(bias_sb[:], bias)
@@ -67,116 +84,111 @@ def tile_attend_gpsqueeze_kernel(tc, tab_words, tab_scales, w1, steep, bias, wo,
         nc.sync.dma_start(og_sb[:], og)
         nc.sync.dma_start(base_sb[:], base)
 
-        slopes = (-1.0 / 64, -0.5, -1.0 / 16, -3.0 / 32)
-        levels = (1.0 / 64, 0.5, 0.0, 1.0 / 32)
-        powers = sb.tile([P, 2, 4], F32, name="powers")
-        line = sb.tile([P, 2, 5], F32, name="line")
-        for n in range(4):
-            nc.gpsimd.memset(powers[:, 0, n : n + 1], slopes[n])
-        nc.scalar.activation(powers[:, 1, 0:2], powers[:, 0, 0:2], ACT.Copy, scale=-1.0)
-        for n in range(2, 4):
-            nc.gpsimd.memset(powers[:, 1, n : n + 1], levels[n])
-        nc.gpsimd.memset(line[:, :, 0:1], 1.0)
+        factors = sb.tile([P, 5], F32, name="factors")
+        nc.gpsimd.memset(factors[:, 0:1], -0.5)
+        nc.scalar.activation(factors[:, 1:2], factors[:, 0:1], ACT.Copy, scale=-1.0)
+        for column, value in ((2, -1.0 / 16), (3, -3.0 / 32), (4, 1.0 / 32)):
+            nc.gpsimd.memset(factors[:, column : column + 1], value)
+        steeps = sb.tile([P, 5], F32, name="steeps")
         half_bias = sb.tile([P, 1], F32, name="half_bias")
-        nc.gpsimd.tensor_scalar(line[:, :, 1:5], powers[:], steep_sb[:], 0.0, ALU.mult, ALU.add)
+        nc.gpsimd.tensor_scalar(steeps[:], factors[:], steep_sb[:], 0.0, ALU.mult, ALU.add)
         nc.gpsimd.tensor_scalar(half_bias[:], bias_sb[:], 0.5, 0.0, ALU.mult, ALU.add)
 
+        picked_words = sb.tile([P, J], U16, name="picked_words", align_bytes=64)
+        picked_bytes = sb.tile([P, J], U8, name="picked_bytes", align_bytes=64)
+        nc.vector.tensor_copy(picked_words[:], words[:].indirect(offsets[:]))
+        nc.vector.tensor_copy(picked_bytes[:], scale_bytes[:].indirect(offsets[:]))
 
-        g_words = sb.tile([P, J], U16, name="g_words", align_bytes=64)
-        g_bytes = sb.tile([P, J], U8, name="g_bytes", align_bytes=64)
-        nc.vector.tensor_copy(g_words[:], words[:].indirect(offsets[:]))
-        nc.vector.tensor_copy(g_bytes[:], sbytes[:].indirect(offsets[:]))
+        def round_on_scalar(rounded, raw):
+            dst, src = interleave_views(rounded, raw)
+            nc.scalar.copy(dst, src)
 
-        def quantise(name, grouped, width):
+        def quantise(name, rounded, width):
             codes = sb.tile([P, width], U32, name=name + "_codes", align_bytes=64)
             scales = sb.tile([P, width], U8, name=name + "_scales", align_bytes=64)
             nc.vector.quantize_mx(
-                out=codes[:].bitcast(FP8X4), scales=scales[:], in_=grouped[:].rearrange("p c t -> p (c t)")
+                out=codes[:].bitcast(FP8X4), scales=scales[:], in_=rounded[:].rearrange("p c t -> p (c t)")
             )
             return codes, scales
 
         w1_bf = sb.tile([P, R, PACK], BF16, name="w1_bf", align_bytes=64)
-        dst, src = interleave_views(w1_bf[:], w1_raw[:])
-        nc.scalar.copy(dst, src)
+        round_on_scalar(w1_bf[:], w1_raw[:])
         w1_codes, w1_scales = quantise("w1", w1_bf, R)
-
-        a_ps = [ps.tile([P, JH], F32, name="a_ps%d" % h) for h in range(HALVES)]
+        a_banks = [ps.tile([P, JH], F32, name="a_bank%d" % h) for h in range(HALVES)]
         for h in range(HALVES):
             cols = slice(h * JH, (h + 1) * JH)
             nc.tensor.matmul_mx(
-                out=a_ps[h][:], lhsT=w1_codes[:].bitcast(FP8X4), lhsT_scale=w1_scales[:],
-                rhs=g_words[:, cols].bitcast(FP4X4), rhs_scale=g_bytes[:, cols], start=True, stop=True,
+                out=a_banks[h][:], lhsT=w1_codes[:].bitcast(FP8X4), lhsT_scale=w1_scales[:],
+                rhs=picked_words[:, cols].bitcast(FP4X4), rhs_scale=picked_bytes[:, cols], start=True, stop=True,
             )
 
-        first_bf = reuse.tile([P, R + JH, PACK], BF16, name="first_bf", align_bytes=64, offset=0)
-
-        def round_on_scalar(grouped, raw):
-            dst, src = interleave_views(grouped, raw)
-            nc.scalar.copy(dst, src)
-
-        round_on_scalar(first_bf[:, R + DY_SHARE[0] : R + JH, :], dy_raw[0][:, :, DY_SHARE[0] : JH])
-        dst, src = interleave_views(first_bf[:, R : R + DY_SHARE[0], :], dy_raw[0][:, :, 0 : DY_SHARE[0]])
+        first_bf = shared.tile([P, R + JH, PACK], BF16, name="first_bf", align_bytes=64, offset=0)
+        round_on_scalar(first_bf[:, R + DY_FIRST_VECTOR : R + JH, :], dy_raw[0][:, :, DY_FIRST_VECTOR:JH])
+        dst, src = interleave_views(first_bf[:, R : R + DY_FIRST_VECTOR, :], dy_raw[0][:, :, 0:DY_FIRST_VECTOR])
         nc.vector.tensor_copy(dst, src)
         round_on_scalar(first_bf[:, 0:R, :], wo_raw[:])
         first_codes, first_scales = quantise("first", first_bf, R + JH)
 
-        def product_with_dy(h, dy_codes, dy_scales):
-            bank = ps.tile([P, JH], F32, name="c_ps%d" % h)
+        def product_with_wo(h, dy_codes, dy_scales):
+            bank = ps.tile([P, JH], F32, name="c_bank%d" % h)
             nc.tensor.matmul_mx(
                 out=bank[:], lhsT=first_codes[:, 0:R].bitcast(FP8X4), lhsT_scale=first_scales[:, 0:R],
                 rhs=dy_codes.bitcast(FP8X4), rhs_scale=dy_scales, start=True, stop=True,
             )
             return bank
 
-        c_banks = [product_with_dy(0, first_codes[:, R : R + JH], first_scales[:, R : R + JH])]
+        c_banks = [product_with_wo(0, first_codes[:, R : R + JH], first_scales[:, R : R + JH])]
 
-        sum_a = reuse.tile([P, G], F32, name="sum_a", align_bytes=64, offset=JH * PACK * 2)
-        a_sb = sb.tile([P, J], F32, name="a_sb", tag="staged", align_bytes=64)
-        for h in range(HALVES):
-            nc.scalar.copy(a_sb[:, h * JH : (h + 1) * JH], a_ps[h][:])
-            nc.vector.tensor_reduce(
-                sum_a[:, h * GH : (h + 1) * GH], a_ps[h][:].rearrange("p (g s) -> p g s", s=S), AX.X, ALU.add
-            )
-        th = reuse.tile([P, G], F32, name="th", align_bytes=64, offset=LATE)
-        nc.scalar.activation(th[:], sum_a[:], ACT.Tanh, bias=half_bias[:], scale=line[:, 1, 4:5])
+        sum_a = shared.tile([P, G], F32, name="sum_a", align_bytes=64, offset=AT_SUM_A)
+        a_sb = sb.tile([P, J], F32, name="a_sb", tag="wo_then_a", align_bytes=64)
+        nc.scalar.copy(a_sb[:, 0:JH], a_banks[0][:])
+        for h in (1, 0):
+            nc.vector.tensor_reduce(sum_a[:, h * GH : (h + 1) * GH], by_group(a_banks[h][:]), AX.X, ALU.add)
+        nc.scalar.copy(a_sb[:, JH:J], a_banks[1][:])
+        th = shared.tile([P, G], F32, name="th", align_bytes=64, offset=AT_TH)
+        nc.scalar.activation(th[:], sum_a[:], ACT.Tanh, bias=half_bias[:], scale=steeps[:, 4:5])
 
-        second_bf = reuse.tile([P, JH, PACK], BF16, name="second_bf", align_bytes=64, offset=0)
+        second_bf = shared.tile([P, JH, PACK], BF16, name="second_bf", align_bytes=64, offset=0)
         nc.gpsimd.tensor_scalar(
-            second_bf[:, 0 : DY_SHARE[1], :], dy_raw[1][:, :, 0 : DY_SHARE[1]].rearrange("p t c -> p c t"),
+            second_bf[:, 0:DY_SECOND_GPSIMD, :], dy_raw[1][:, :, 0:DY_SECOND_GPSIMD].rearrange("p t c -> p c t"),
             1.0, 0.0, ALU.mult, ALU.add,
         )
-        round_on_scalar(second_bf[:, DY_SHARE[1] : JH, :], dy_raw[1][:, :, DY_SHARE[1] : JH])
+        gained = shared.tile([P, 2], F32, name="gained", align_bytes=64, offset=AT_GAINED)
+        nc.gpsimd.tensor_scalar(gained[:], steeps[:, 0:2], og_sb[:], 1.0 / 32, ALU.mult, ALU.mult)
+        round_on_scalar(second_bf[:, DY_SECOND_GPSIMD:JH, :], dy_raw[1][:, :, DY_SECOND_GPSIMD:JH])
         second_codes, second_scales = quantise("second", second_bf, JH)
-        c_banks.append(product_with_dy(1, second_codes[:], second_scales[:]))
+        c_banks.append(product_with_wo(1, second_codes[:], second_scales[:]))
 
-        gate = sb.tile([P, 7, G], F32, name="gate")
+        th2 = sb.tile([P, G], F32, name="th2")
+        common = sb.tile([P, G], F32, name="common")
+        to_gain = sb.tile([P, 2, G], F32, name="to_gain")
+        to_shift = sb.tile([P, 2, G], F32, name="to_shift")
         coef = sb.tile([P, 6, G], F32, name="coef")
-        for n in range(5):
-            nc.scalar.activation(
-                gate[:, 2 + n, :], th[:], ACT.Identity, bias=line[:, 1, n : n + 1], scale=line[:, 0, n : n + 1]
-            )
-        nc.vector.tensor_tensor(
-            gate[:, 0:2, :], gate[:, 3:5, :], gate[:, 2:3, :].to_broadcast([P, 2, G]), ALU.mult
+        nc.scalar.activation(th2[:], th[:], ACT.Square)
+        nc.scalar.activation(to_gain[:, 1, :], th[:], ACT.Copy, bias=1.0)
+        nc.scalar.activation(to_gain[:, 0, :], th2[:], ACT.Identity, bias=steeps[:, 1:2], scale=steeps[:, 0:1])
+        nc.scalar.activation(common[:], th2[:], ACT.Identity, bias=gained[:, 1:2], scale=gained[:, 0:1])
+        nc.scalar.activation(to_shift[:, 0, :], th[:], ACT.Copy, scale=steeps[:, 2:3])
+        nc.scalar.activation(to_shift[:, 1, :], th[:], ACT.Identity, bias=steeps[:, 4:5], scale=steeps[:, 3:4])
+        nc.gpsimd.tensor_tensor(
+            coef[:, 2:4, :], to_gain[:], common[:].unsqueeze(1).to_broadcast([P, 2, G]), ALU.mult
         )
-        nc.vector.scalar_tensor_tensor(
-            coef[:, 2:4, :], gate[:, 1:3, :], og_sb[:], gate[:, 0:1, :].to_broadcast([P, 2, G]), ALU.mult, ALU.mult
-        )
-        nc.vector.tensor_tensor(coef[:, 0:2, :], coef[:, 2:4, :], gate[:, 5:7, :], ALU.mult)
+        nc.gpsimd.tensor_tensor(coef[:, 0:2, :], coef[:, 2:4, :], to_shift[:], ALU.mult)
 
         sums = sb.tile([P, 3, G], F32, name="sums")
-        c_grouped = []
         squares = []
         for h in range(HALVES):
-            cols = slice(h * JH, (h + 1) * JH)
             groups = slice(h * GH, (h + 1) * GH)
-            c_ps = c_banks[h]
-            c_grouped.append(c_ps[:].rearrange("p (g s) -> p g s", s=S))
-            squares.append(reuse.tile([P, JH], F32, name="squares%d" % h, align_bytes=64, offset=LATE + (1 - h) * JH * 4))
-            prods = sb.tile([P, JH], F32, name="prods%d" % h)
-            nc.vector.tensor_tensor(prods[:], c_ps[:], a_sb[:, cols], ALU.mult)
-            nc.vector.tensor_reduce(sums[:, 2, groups], c_grouped[h], AX.X, ALU.add)
-            nc.scalar.activation(squares[h][:], c_ps[:], ACT.Square)
-            nc.vector.tensor_reduce(sums[:, 1, groups], prods[:].rearrange("p (g s) -> p g s", s=S), AX.X, ALU.add)
+            squares.append(
+                shared.tile(
+                    [P, JH], F32, name="squares%d" % h, align_bytes=64, offset=AT_SQUARES + h * SQUARES_BYTES
+                )
+            )
+            products = sb.tile([P, JH], F32, name="products%d" % h)
+            nc.vector.tensor_tensor(products[:], c_banks[h][:], a_sb[:, h * JH : (h + 1) * JH], ALU.mult)
+            nc.vector.tensor_reduce(sums[:, 2, groups], by_group(c_banks[h][:]), AX.X, ALU.add)
+            nc.scalar.activation(squares[h][:], c_banks[h][:], ACT.Square)
+            nc.vector.tensor_reduce(sums[:, 1, groups], by_group(products[:]), AX.X, ALU.add)
 
         terms = sb.tile([P, 2, 2, G], F32, name="terms")
         nc.vector.tensor_tensor(
@@ -187,26 +199,45 @@ def tile_attend_gpsqueeze_kernel(tc, tab_words, tab_scales, w1, steep, bias, wo,
         )
         nc.vector.tensor_tensor(coef[:, 4:6, :], terms[:, :, 0, :], terms[:, :, 1, :], ALU.add)
         for h in range(HALVES):
-            nc.vector.tensor_reduce(
-                sums[:, 0, h * GH : (h + 1) * GH], squares[h][:].rearrange("p (g s) -> p g s", s=S), AX.X, ALU.add
-            )
+            nc.vector.tensor_reduce(sums[:, 0, h * GH : (h + 1) * GH], by_group(squares[h][:]), AX.X, ALU.add)
         parts = sb.tile([P, 2, G], F32, name="parts")
         nc.vector.tensor_tensor(parts[:], coef[:, 3:5, :], sums[:, 0:2, :], ALU.mult)
+        gain = coef[:, 5, :]
+
+        groups_vector = G - GROUPS_SCALAR
+        in_bank0 = GH - GROUPS_SCALAR
+        scaled = sb.tile([P, groups_vector, S], F32, name="scaled")
+        nc.vector.tensor_tensor(
+            scaled[:, 0:in_bank0, :], by_group(c_banks[0][:])[:, GROUPS_SCALAR:GH, :],
+            over_slots(gain[:, GROUPS_SCALAR:GH], in_bank0), ALU.mult,
+        )
+        nc.vector.tensor_tensor(
+            scaled[:, in_bank0:groups_vector, :], by_group(c_banks[1][:]), over_slots(gain[:, GH:G], GH), ALU.mult
+        )
         shift = sb.tile([P, G], F32, name="shift")
         nc.vector.tensor_tensor(shift[:], parts[:, 0, :], parts[:, 1, :], ALU.add)
-        for h in range(HALVES):
-            cols = slice(h * JH, (h + 1) * JH)
-            groups = slice(h * GH, (h + 1) * GH)
-            scaled = sb.tile([P, GH, S], F32, name="scaled%d" % h)
-            based = sb.tile([P, GH, S], F32, name="based%d" % h)
-            result = sb.tile([P, GH, S], F32, name="result%d" % h)
-            nc.vector.tensor_tensor(
-                scaled[:], c_grouped[h], coef[:, 5, groups].unsqueeze(2).to_broadcast([P, GH, S]), ALU.mult
+        affine = sb.tile([P, GROUPS_SCALAR, S], F32, name="affine")
+        for g in range(GROUPS_SCALAR):
+            nc.scalar.activation(
+                affine[:, g, :], by_group(c_banks[0][:])[:, g, :], ACT.Identity,
+                bias=shift[:, g : g + 1], scale=gain[:, g : g + 1],
             )
+        base_grouped = by_group(base_sb[:])
+        based = sb.tile([P, groups_vector, S], F32, name="based")
+        result_vector = sb.tile([P, groups_vector, S], F32, name="result_vector")
+        result_scalar = sb.tile([P, GROUPS_SCALAR, S], F32, name="result_scalar")
+        run = groups_vector // 2
+        for lo in (0, run):
+            first = GROUPS_SCALAR + lo
             nc.vector.tensor_tensor(
-                based[:], scaled[:], base_sb[:, cols].rearrange("p (g s) -> p g s", s=S), ALU.add
+                based[:, lo : lo + run, :], scaled[:, lo : lo + run, :], base_grouped[:, first : first + run, :], ALU.add
             )
+        for lo in (0, run):
+            first = GROUPS_SCALAR + lo
             nc.vector.tensor_tensor(
-                result[:], based[:], shift[:, groups].unsqueeze(2).to_broadcast([P, GH, S]), ALU.add
+                result_vector[:, lo : lo + run, :], based[:, lo : lo + run, :],
+                over_slots(shift[:, first : first + run], run), ALU.add,
             )
-            nc.sync.dma_start(out[:, cols], result[:].rearrange("p g s -> p (g s)"))
+        nc.sync.dma_start(out[:, GROUPS_SCALAR * S : J], result_vector[:].rearrange("p g s -> p (g s)"))
+        nc.vector.tensor_tensor(result_scalar[:], affine[:], base_grouped[:, 0:GROUPS_SCALAR, :], ALU.add)
+        nc.sync.dma_start(out[:, 0 : GROUPS_SCALAR * S], result_scalar[:].rearrange("p g s -> p (g s)"))

from contextlib import ExitStack

import concourse.mybir as mybir

K, R, F, T, J, G = 512, 128, 512, 2048, 512, 32
FLOPS = 2 * K * R * J + 2 * F * R * J

F32 = mybir.dt.float32
BF16 = mybir.dt.bfloat16
I32 = mybir.dt.int32
U32 = mybir.dt.uint32
U16 = mybir.dt.uint16
U8 = mybir.dt.uint8
FP8X4 = mybir.dt.float8_e4m3fn_x4
FP4X4 = mybir.dt.float4_e2m1fn_x4
ACT = mybir.ActivationFunctionType
ALU = mybir.AluOpType
AX = mybir.AxisListType

P = 128
PACK = 4
S = J // G
HALVES = 2
JH = J // HALVES
GH = G // HALVES
DY_FIRST_VECTOR = 128
DY_SECOND_GPSIMD = 160
GROUPS_SCALAR = 12

FIRST_BF_BYTES = (R + JH) * PACK * 2
SECOND_BF_BYTES = JH * PACK * 2
SQUARES_BYTES = JH * 4
AT_SUM_A = SECOND_BF_BYTES
AT_GAINED = AT_SUM_A + G * 4
AT_SQUARES = FIRST_BF_BYTES
AT_TH = AT_SQUARES + SQUARES_BYTES - G * 2


def interleave_views(rounded, raw):
    return (
        rounded.rearrange("p (c i) t -> p c t i", i=4),
        raw.rearrange("p t (c i) -> p c t i", i=4),
    )


def by_group(flat):
    return flat.rearrange("p (g s) -> p g s", s=S)


def over_slots(per_group, count):
    return per_group.unsqueeze(2).to_broadcast([P, count, S])


def tile_attend_gpsqueeze_kernel(tc, tab_words, tab_scales, w1, steep, bias, wo, dy, og, base, offs, out):
    nc = tc.nc
    with ExitStack() as ctx:
        sb = ctx.enter_context(tc.tile_pool(name="sb", bufs=1))
        shared = ctx.enter_context(tc.tile_pool(name="shared", bufs=1))
        ps = ctx.enter_context(tc.psum_pool(name="ps", bufs=1))

        offsets = sb.tile([P, J // 16], U16, name="offsets")
        words = sb.tile([P, T], U16, name="words", align_bytes=64)
        scale_bytes = sb.tile([P, T], U8, name="scale_bytes", align_bytes=64)
        w1_raw = sb.tile([P, PACK, R], F32, name="w1_raw", align_bytes=64)
        wo_raw = sb.tile([P, PACK, R], F32, name="wo_raw", tag="wo_then_a", align_bytes=64)
        dy_raw = [sb.tile([P, PACK, JH], F32, name="dy_raw%d" % h, align_bytes=64) for h in range(HALVES)]
        base_sb = sb.tile([P, J], F32, name="base_sb", align_bytes=64)
        steep_sb = sb.tile([P, 1], F32, name="steep_sb")
        bias_sb = sb.tile([P, 1], F32, name="bias_sb")
        og_sb = sb.tile([P, 1], F32, name="og_sb")

        nc.vector.memset(scale_bytes[:].bitcast(I32), 0)
        nc.sync.dma_start(words[:].bitcast(I32), tab_words[0].bitcast(I32))
        nc.sync.dma_start(offsets[:], offs)
        for r in range(4):
            nc.sync.dma_start(scale_bytes[r:P:32, :].bitcast(I32), tab_scales[0][r:16:4, :].bitcast(I32))
        nc.sync.dma_start(w1_raw[:], w1.rearrange("(p t) r -> p t r", t=PACK))
        nc.gpsimd.dma_start(steep_sb[:], steep)
        nc.gpsimd.dma_start(bias_sb[:], bias)
        dy_view = dy.rearrange("(p t) j -> p t j", t=PACK)
        nc.sync.dma_start(dy_raw[0][:], dy_view[:, :, 0:JH])
        nc.sync.dma_start(wo_raw[:], wo.rearrange("(p t) r -> p t r", t=PACK))
        nc.sync.dma_start(dy_raw[1][:], dy_view[:, :, JH:J])
        nc.sync.dma_start(og_sb[:], og)
        nc.sync.dma_start(base_sb[:], base)

        factors = sb.tile([P, 5], F32, name="factors")
        nc.gpsimd.memset(factors[:, 0:1], -0.5)
        nc.scalar.activation(factors[:, 1:2], factors[:, 0:1], ACT.Copy, scale=-1.0)
        for column, value in ((2, -1.0 / 16), (3, -3.0 / 32), (4, 1.0 / 32)):
            nc.gpsimd.memset(factors[:, column : column + 1], value)
        steeps = sb.tile([P, 5], F32, name="steeps")
        half_bias = sb.tile([P, 1], F32, name="half_bias")
        nc.gpsimd.tensor_scalar(steeps[:], factors[:], steep_sb[:], 0.0, ALU.mult, ALU.add)
        nc.gpsimd.tensor_scalar(half_bias[:], bias_sb[:], 0.5, 0.0, ALU.mult, ALU.add)

        picked_words = sb.tile([P, J], U16, name="picked_words", align_bytes=64)
        picked_bytes = sb.tile([P, J], U8, name="picked_bytes", align_bytes=64)
        nc.vector.tensor_copy(picked_words[:], words[:].indirect(offsets[:]))
        nc.vector.tensor_copy(picked_bytes[:], scale_bytes[:].indirect(offsets[:]))

        def round_on_scalar(rounded, raw):
            dst, src = interleave_views(rounded, raw)
            nc.scalar.copy(dst, src)

        def quantise(name, rounded, width):
            codes = sb.tile([P, width], U32, name=name + "_codes", align_bytes=64)
            scales = sb.tile([P, width], U8, name=name + "_scales", align_bytes=64)
            nc.vector.quantize_mx(
                out=codes[:].bitcast(FP8X4), scales=scales[:], in_=rounded[:].rearrange("p c t -> p (c t)")
            )
            return codes, scales

        w1_bf = sb.tile([P, R, PACK], BF16, name="w1_bf", align_bytes=64)
        round_on_scalar(w1_bf[:], w1_raw[:])
        w1_codes, w1_scales = quantise("w1", w1_bf, R)
        a_banks = [ps.tile([P, JH], F32, name="a_bank%d" % h) for h in range(HALVES)]
        for h in range(HALVES):
            cols = slice(h * JH, (h + 1) * JH)
            nc.tensor.matmul_mx(
                out=a_banks[h][:], lhsT=w1_codes[:].bitcast(FP8X4), lhsT_scale=w1_scales[:],
                rhs=picked_words[:, cols].bitcast(FP4X4), rhs_scale=picked_bytes[:, cols], start=True, stop=True,
            )

        first_bf = shared.tile([P, R + JH, PACK], BF16, name="first_bf", align_bytes=64, offset=0)
        round_on_scalar(first_bf[:, R + DY_FIRST_VECTOR : R + JH, :], dy_raw[0][:, :, DY_FIRST_VECTOR:JH])
        dst, src = interleave_views(first_bf[:, R : R + DY_FIRST_VECTOR, :], dy_raw[0][:, :, 0:DY_FIRST_VECTOR])
        nc.vector.tensor_copy(dst, src)
        round_on_scalar(first_bf[:, 0:R, :], wo_raw[:])
        first_codes, first_scales = quantise("first", first_bf, R + JH)

        def product_with_wo(h, dy_codes, dy_scales):
            bank = ps.tile([P, JH], F32, name="c_bank%d" % h)
            nc.tensor.matmul_mx(
                out=bank[:], lhsT=first_codes[:, 0:R].bitcast(FP8X4), lhsT_scale=first_scales[:, 0:R],
                rhs=dy_codes.bitcast(FP8X4), rhs_scale=dy_scales, start=True, stop=True,
            )
            return bank

        c_banks = [product_with_wo(0, first_codes[:, R : R + JH], first_scales[:, R : R + JH])]

        sum_a = shared.tile([P, G], F32, name="sum_a", align_bytes=64, offset=AT_SUM_A)
        a_sb = sb.tile([P, J], F32, name="a_sb", tag="wo_then_a", align_bytes=64)
        nc.scalar.copy(a_sb[:, 0:JH], a_banks[0][:])
        for h in (1, 0):
            nc.vector.tensor_reduce(sum_a[:, h * GH : (h + 1) * GH], by_group(a_banks[h][:]), AX.X, ALU.add)
        nc.scalar.copy(a_sb[:, JH:J], a_banks[1][:])
        th = shared.tile([P, G], F32, name="th", align_bytes=64, offset=AT_TH)
        nc.scalar.activation(th[:], sum_a[:], ACT.Tanh, bias=half_bias[:], scale=steeps[:, 4:5])

        second_bf = shared.tile([P, JH, PACK], BF16, name="second_bf", align_bytes=64, offset=0)
        nc.gpsimd.tensor_scalar(
            second_bf[:, 0:DY_SECOND_GPSIMD, :], dy_raw[1][:, :, 0:DY_SECOND_GPSIMD].rearrange("p t c -> p c t"),
            1.0, 0.0, ALU.mult, ALU.add,
        )
        gained = shared.tile([P, 2], F32, name="gained", align_bytes=64, offset=AT_GAINED)
        nc.gpsimd.tensor_scalar(gained[:], steeps[:, 0:2], og_sb[:], 1.0 / 32, ALU.mult, ALU.mult)
        round_on_scalar(second_bf[:, DY_SECOND_GPSIMD:JH, :], dy_raw[1][:, :, DY_SECOND_GPSIMD:JH])
        second_codes, second_scales = quantise("second", second_bf, JH)
        c_banks.append(product_with_wo(1, second_codes[:], second_scales[:]))

        th2 = sb.tile([P, G], F32, name="th2")
        common = sb.tile([P, G], F32, name="common")
        to_gain = sb.tile([P, 2, G], F32, name="to_gain")
        to_shift = sb.tile([P, 2, G], F32, name="to_shift")
        coef = sb.tile([P, 6, G], F32, name="coef")
        nc.scalar.activation(th2[:], th[:], ACT.Square)
        nc.scalar.activation(to_gain[:, 1, :], th[:], ACT.Copy, bias=1.0)
        nc.scalar.activation(to_gain[:, 0, :], th2[:], ACT.Identity, bias=steeps[:, 1:2], scale=steeps[:, 0:1])
        nc.scalar.activation(common[:], th2[:], ACT.Identity, bias=gained[:, 1:2], scale=gained[:, 0:1])
        nc.scalar.activation(to_shift[:, 0, :], th[:], ACT.Copy, scale=steeps[:, 2:3])
        nc.scalar.activation(to_shift[:, 1, :], th[:], ACT.Identity, bias=steeps[:, 4:5], scale=steeps[:, 3:4])
        nc.gpsimd.tensor_tensor(
            coef[:, 2:4, :], to_gain[:], common[:].unsqueeze(1).to_broadcast([P, 2, G]), ALU.mult
        )
        nc.gpsimd.tensor_tensor(coef[:, 0:2, :], coef[:, 2:4, :], to_shift[:], ALU.mult)

        sums = sb.tile([P, 3, G], F32, name="sums")
        squares = []
        for h in range(HALVES):
            groups = slice(h * GH, (h + 1) * GH)
            squares.append(
                shared.tile(
                    [P, JH], F32, name="squares%d" % h, align_bytes=64, offset=AT_SQUARES + h * SQUARES_BYTES
                )
            )
            products = sb.tile([P, JH], F32, name="products%d" % h)
            nc.vector.tensor_tensor(products[:], c_banks[h][:], a_sb[:, h * JH : (h + 1) * JH], ALU.mult)
            nc.vector.tensor_reduce(sums[:, 2, groups], by_group(c_banks[h][:]), AX.X, ALU.add)
            nc.scalar.activation(squares[h][:], c_banks[h][:], ACT.Square)
            nc.vector.tensor_reduce(sums[:, 1, groups], by_group(products[:]), AX.X, ALU.add)

        terms = sb.tile([P, 2, 2, G], F32, name="terms")
        nc.vector.tensor_tensor(
            terms[:],
            coef[:, 0:4, :].rearrange("p (o i) g -> p o i g", i=2),
            sums[:, 1:3, :].unsqueeze(1).to_broadcast([P, 2, 2, G]),
            ALU.mult,
        )
        nc.vector.tensor_tensor(coef[:, 4:6, :], terms[:, :, 0, :], terms[:, :, 1, :], ALU.add)
        for h in range(HALVES):
            nc.vector.tensor_reduce(sums[:, 0, h * GH : (h + 1) * GH], by_group(squares[h][:]), AX.X, ALU.add)
        parts = sb.tile([P, 2, G], F32, name="parts")
        nc.vector.tensor_tensor(parts[:], coef[:, 3:5, :], sums[:, 0:2, :], ALU.mult)
        gain = coef[:, 5, :]

        groups_vector = G - GROUPS_SCALAR
        in_bank0 = GH - GROUPS_SCALAR
        scaled = sb.tile([P, groups_vector, S], F32, name="scaled")
        nc.vector.tensor_tensor(
            scaled[:, 0:in_bank0, :], by_group(c_banks[0][:])[:, GROUPS_SCALAR:GH, :],
            over_slots(gain[:, GROUPS_SCALAR:GH], in_bank0), ALU.mult,
        )
        nc.vector.tensor_tensor(
            scaled[:, in_bank0:groups_vector, :], by_group(c_banks[1][:]), over_slots(gain[:, GH:G], GH), ALU.mult
        )
        shift = sb.tile([P, G], F32, name="shift")
        nc.vector.tensor_tensor(shift[:], parts[:, 0, :], parts[:, 1, :], ALU.add)
        affine = sb.tile([P, GROUPS_SCALAR, S], F32, name="affine")
        for g in range(GROUPS_SCALAR):
            nc.scalar.activation(
                affine[:, g, :], by_group(c_banks[0][:])[:, g, :], ACT.Identity,
                bias=shift[:, g : g + 1], scale=gain[:, g : g + 1],
            )
        base_grouped = by_group(base_sb[:])
        based = sb.tile([P, groups_vector, S], F32, name="based")
        result_vector = sb.tile([P, groups_vector, S], F32, name="result_vector")
        result_scalar = sb.tile([P, GROUPS_SCALAR, S], F32, name="result_scalar")
        run = groups_vector // 2
        for lo in (0, run):
            first = GROUPS_SCALAR + lo
            nc.vector.tensor_tensor(
                based[:, lo : lo + run, :], scaled[:, lo : lo + run, :], base_grouped[:, first : first + run, :], ALU.add
            )
        for lo in (0, run):
            first = GROUPS_SCALAR + lo
            nc.vector.tensor_tensor(
                result_vector[:, lo : lo + run, :], based[:, lo : lo + run, :],
                over_slots(shift[:, first : first + run], run), ALU.add,
            )
        nc.sync.dma_start(out[:, GROUPS_SCALAR * S : J], result_vector[:].rearrange("p g s -> p (g s)"))
        nc.vector.tensor_tensor(result_scalar[:], affine[:], base_grouped[:, 0:GROUPS_SCALAR, :], ALU.add)
        nc.sync.dma_start(out[:, 0 : GROUPS_SCALAR * S], result_scalar[:].rearrange("p g s -> p (g s)"))
